import numpy as np
import ml_dtypes


def mxq(x, axis, fmt="e4m3"):
    dtype, down = {"e4m3": (ml_dtypes.float8_e4m3fn, 7), "e5m2": (ml_dtypes.float8_e5m2, 14)}[fmt]
    v = np.moveaxis(np.asarray(x, np.float32).astype(ml_dtypes.bfloat16).astype(np.float64), axis, -1)
    blocks = v.reshape(v.shape[:-1] + (-1, 32))
    amax = np.abs(blocks).max(-1, keepdims=True)
    byte = np.maximum(np.where(amax > 0, np.frexp(amax)[1] - 1 + 127, 0) - down, 1)
    scale = np.exp2(byte - 127.0)
    codes = (blocks / scale).astype(np.float32).astype(dtype).astype(np.float64)
    return np.moveaxis((codes * scale).reshape(v.shape), -1, axis)


WIDE = False


def mx_kscale(k):
    if not WIDE:
        return np.ones(k)
    levels = np.array([10, -10, 5, -5, 0])
    if k % 512:
        return np.exp2(np.random.permutation(np.resize(levels, k // 32))).repeat(32)
    a = np.empty((k // 512, 16))
    for p in range(k // 512):
        a[p, :8] = np.random.permutation(np.resize(levels, 8))
        for g in range(8):
            far = levels[np.abs(levels - a[p, g]) >= 10]
            a[p, g + 8] = far[np.random.randint(len(far))]
    return np.exp2(a.ravel()).repeat(32)


def f64(x):
    return np.asarray(x).astype(np.float64)


def striped(idx):
    return np.tile(np.asarray(idx).reshape(-1, 16).T, (8, 1)).astype(np.uint16)


def unstriped(offs):
    return offs[:16].T.reshape(-1).astype(np.int64)


E2M1 = np.array([0.0, 0.5, 1.0, 1.5, 2.0, 3.0, 4.0, 6.0, -0.0, -0.5, -1.0, -1.5, -2.0, -3.0, -4.0, -6.0])


def pack_weight(w, fmt):
    k, n = w.shape
    w = f64(np.asarray(w, np.float32).astype(ml_dtypes.bfloat16)).reshape(k // 32, 32, n)
    amax = np.abs(w).max(1)
    if fmt == "e4m3":
        byte = np.frexp(amax)[1] - 1 + 127 - 7
    else:
        mant, ex = np.frexp(amax / 6.0)
        byte = np.where(mant > 0.5, ex, ex - 1) + 127
    byte = np.clip(np.where(amax > 0, byte, 1), 1, 254)
    scaled = (w * np.exp2(127.0 - byte)[:, None, :]).reshape(k, n).astype(np.float32)
    by_word = np.ascontiguousarray(scaled.reshape(k // 512, 128, 4, n).transpose(0, 1, 3, 2))
    if fmt == "e4m3":
        words = by_word.astype(ml_dtypes.float8_e4m3fn).view(np.uint8)
    else:
        c = by_word.astype(ml_dtypes.float4_e2m1fn).view(np.uint8) & 0xF
        words = (c[..., 0::2] | (c[..., 1::2] << 4)).reshape(k // 512, 128, 2 * n)
    return np.ascontiguousarray(words), np.ascontiguousarray(byte.astype(np.uint8).reshape(k // 512, 16, n))


def unpack_weight(words, scales, fmt):
    g, _, n = scales.shape
    words = np.ascontiguousarray(words).reshape(g, 128, n, -1)
    if fmt == "e4m3":
        vals = words.view(ml_dtypes.float8_e4m3fn).astype(np.float64)
    else:
        nib = np.empty((g, 128, n, 4), np.uint8)
        nib[..., 0::2] = words & 0xF
        nib[..., 1::2] = words >> 4
        vals = E2M1[nib]
    vals = vals * np.repeat(np.exp2(scales.astype(np.float64) - 127.0), 8, axis=1)[..., None]
    return vals.transpose(0, 1, 3, 2).reshape(g * 512, n)


def sigmoid(v):
    return 1.0 / (1.0 + np.exp(-v))


D, E, T, I, Q, G, U = 512, 512, 1024, 256, 512, 16, 1024


def setup_inputs():
    n = np.random.standard_normal
    idx = np.random.permutation(T)[:I]
    idx4 = np.random.permutation(U)[:I]
    fd = mx_kscale(D)
    fe = mx_kscale(E)
    fq = mx_kscale(Q)
    keysp = pack_weight(n((D, T)) / fd[:, None], "e2m1")
    valsp = pack_weight(n((E, T)) / fe[:, None], "e2m1")
    return {
        "query": (n((D, Q)) * 0.5 / np.sqrt(D) * fd[:, None]).astype(np.float32),
        "keys_words": keysp[0],
        "keys_scales": keysp[1],
        "helpf": (np.random.uniform(0.5, 1.5, (Q, 1))).astype(np.float32),
        "gout": (n((E, Q)) * 1 / np.sqrt(E) * fe[:, None]).astype(np.float32),
        "vals_words": valsp[0],
        "vals_scales": valsp[1],
        "qs": (np.random.uniform(100.0, 400.0, (Q, 1)) * fq[:, None]).astype(np.float32),
        "qrows": (n((Q, D)) / fq[:, None]).astype(np.float32),
        "old": (n((D, U)) * 4.0).astype(np.float32),
        "fade": (np.random.uniform(0.5, 1.0, (1, U))).astype(np.float32),
        "offs": striped(idx),
        "offs4": striped(idx4),
    }


def reference(query, keys_words, keys_scales, helpf, gout, vals_words, vals_scales, qs, qrows, old, fade, offs, offs4):
    idx = unstriped(offs)
    idx4 = unstriped(offs4)
    keysu = unpack_weight(keys_words, keys_scales, "e2m1")
    valsu = unpack_weight(vals_words, vals_scales, "e2m1")
    queryq = mxq(f64(query), 0, "e4m3")
    keysidxg = keysu[:, idx]
    a = queryq.T @ keysidxg
    m1 = a.reshape(Q, G, I // G).mean(axis=2)
    gt = sigmoid(m1 * 4.0)
    gr = np.repeat(gt, I // G, axis=1)
    s = a * (gr * f64(helpf) + 1.0)
    p = np.exp(s - np.max(s, axis=1, keepdims=True))
    z = np.sum(p, axis=1, keepdims=True)
    goutq = mxq(f64(gout), 0, "e4m3")
    valsidxg = valsu[:, idx]
    c0 = goutq.T @ valsidxg
    dz = np.sum(c0 * p / np.square(z) * (-1.0), axis=1, keepdims=True)
    dp = c0 / z + dz
    ds = dp * p
    dgr = ds * a * f64(helpf)
    dgt = dgr.reshape(Q, G, I // G).sum(axis=2)
    dm1 = dgt * gt * (1.0 - gt) * 4.0
    e1 = dm1 / 16.0
    r1 = np.repeat(e1, I // G, axis=1)
    da = ds * (gr * f64(helpf) + 1.0) + r1
    gs = da * f64(qs)
    qrowsq = mxq(f64(qrows), 0, "e4m3")
    gsq = mxq(gs, 0, "e4m3")
    gk = qrowsq.T @ gsq
    gf = np.zeros((D, U))
    gf[:, idx4] = gk
    y = f64(old) * f64(fade) + gf
    return y

@@ -1,0 +1,292 @@
+from contextlib import ExitStack
+
+import concourse.mybir as mybir
+from concourse.masks import make_identity
+
+D, E, T, I, Q, G, U = 512, 512, 1024, 256, 512, 16, 1024
+FLOPS = 3 * 2 * 512 * 512 * 256
+
+F32 = mybir.dt.float32
+BF16 = mybir.dt.bfloat16
+I32 = mybir.dt.int32
+U32 = mybir.dt.uint32
+U16 = mybir.dt.uint16
+U8 = mybir.dt.uint8
+FP8X4 = mybir.dt.float8_e4m3fn_x4
+FP4X4 = mybir.dt.float4_e2m1fn_x4
+ALU = mybir.AluOpType
+ACT = mybir.ActivationFunctionType
+AX = mybir.AxisListType
+
+P = 128
+PACK = 4
+PAGE = I // G
+HALVES = 2
+PAIR = 2
+SCALAR_PAGES = 0
+FADE_COLS = 256
+GPSIMD_ADD_TILES = 2
+
+
+def tile_attend_bpagemates_k_kernel(tc, query, keys_words, keys_scales, helpf, gout, vals_words, vals_scales,
+                                     qs, qrows, old, fade, offs, offs4, out):
+    nc = tc.nc
+    with ExitStack() as ctx:
+        lists = ctx.enter_context(tc.tile_pool(name="lists", bufs=1))
+        sb = ctx.enter_context(tc.tile_pool(name="sb", bufs=1))
+        ps = ctx.enter_context(tc.psum_pool(name="ps", bufs=1))
+
+        def new_tile(name, shape, dtype, tag=None):
+            return sb.tile(shape, dtype, name=name, tag=tag or name, align_bytes=64)
+
+        slots = lists.tile([P, I // 16], U16, name="slots")
+        places = lists.tile([P, I // 16], U16, name="places")
+
+        key_bytes = new_tile("key_bytes", [P, T], U8)
+        val_bytes = new_tile("val_bytes", [P, T], U8)
+        windows = [new_tile("window%d" % c, [P, U], F32) for c in range(D // P)]
+        for window in windows:
+            nc.vector.memset(window[:], 0.0)
+
+        def load_bytes(plane, scales):
+            for quad in range(4):
+                rows = scales[0, 4 * quad:4 * quad + 4, :].bitcast(I32)
+                nc.sync.dma_start(out=plane[32 * quad:32 * quad + 32, :].bitcast(I32),
+                                  in_=rows.unsqueeze(0).to_broadcast([8, 4, T // 4]))
+
+        nc.sync.dma_start(slots[:], offs)
+        key_words = new_tile("key_words", [P, T], U16)
+        nc.sync.dma_start(out=key_words[:].bitcast(I32), in_=keys_words[0].bitcast(I32))
+        load_bytes(key_bytes, keys_scales)
+        val_words = new_tile("val_words", [P, T], U16)
+        nc.sync.dma_start(out=val_words[:].bitcast(I32), in_=vals_words[0].bitcast(I32))
+        query_raw = new_tile("query_raw", [P, PACK, Q], F32)
+        nc.sync.dma_start(out=query_raw[:], in_=query.rearrange("(p j) q -> p j q", j=PACK))
+        help_col = new_tile("help_col", [P, PACK], F32)
+        nc.sync.dma_start(out=help_col[:], in_=helpf.rearrange("(p r) o -> p (r o)", r=PACK))
+        load_bytes(val_bytes, vals_scales)
+        fade_col = new_tile("fade_col", [P, U // P], F32)
+        nc.sync.dma_start(out=fade_col[:], in_=fade.rearrange("o (n m) -> (o n) m", n=P))
+        gout_raw = new_tile("gout_raw", [P, PACK, Q], F32)
+        nc.sync.dma_start(out=gout_raw[:], in_=gout.rearrange("(p j) q -> p j q", j=PACK))
+        qs_col = new_tile("qs_col", [P, PACK], F32)
+        nc.sync.dma_start(out=qs_col[:], in_=qs.rearrange("(p r) o -> p (r o)", r=PACK))
+        olds = [new_tile("old%d" % c, [P, U], F32) for c in range(D // P)]
+        for c in range(D // P):
+            nc.sync.dma_start(out=olds[c][:], in_=old[c * P:(c + 1) * P, :])
+        qrows_raw = new_tile("qrows_raw", [P, PACK, D], F32)
+        nc.sync.dma_start(out=qrows_raw[:], in_=qrows.rearrange("(p r) d -> p r d", r=PACK))
+        nc.sync.dma_start(places[:], offs4)
+
+        half_help = new_tile("half_help", [P, PACK], F32, tag="gout_dealt0")
+        half_help1 = new_tile("half_help1", [P, PACK], F32)
+        nc.scalar.activation(out=half_help[:], in_=help_col[:], func=ACT.Copy, scale=0.5)
+        nc.scalar.activation(out=half_help1[:], in_=help_col[:], func=ACT.Copy, scale=0.5, bias=1.0)
+
+        ident = new_tile("ident", [P, P], F32)
+        make_identity(nc, ident[:])
+        fade_rows = new_tile("fade_rows", [P, U], F32)
+        for b in range(2):
+            bank = ps.tile([P, 4, P], F32, name="fade_bank%d" % b)
+            for m in range(4):
+                col = 4 * b + m
+                nc.tensor.transpose(bank[:, m, :], fade_col[:, col:col + 1].to_broadcast([P, P]), ident[:])
+            nc.scalar.copy(out=fade_rows[:].rearrange("p (n m) -> p n m", n=P)[:, :, 4 * b:4 * b + 4],
+                           in_=bank[:].rearrange("p m n -> p n m"))
+
+        def gather(name, words, plane):
+            picked_words = new_tile(name + "_picked_words", [P, I], U16)
+            picked_bytes = new_tile(name + "_picked_bytes", [P, I], U8)
+            nc.vector.tensor_copy(picked_words[:], words[:].indirect(slots[:]))
+            nc.vector.tensor_copy(picked_bytes[:], plane[:].indirect(slots[:]))
+            return picked_words, picked_bytes
+
+        def deal(name, raw, half, copy, tag=None):
+            dealt = new_tile("%s_dealt%d" % (name, half), [P, PAIR, P, PACK], BF16, tag=tag)
+            rows = raw[:].rearrange("p j (s r) -> p s j r", r=PACK)[:, :, :, PAIR * half:PAIR * (half + 1)]
+            copy(out=dealt[:].rearrange("p r s j -> p s j r"), in_=rows)
+            return dealt[:].rearrange("p r s j -> p (r s j)")
+
+        def quantize(name, values):
+            width = values.shape[1] // PACK
+            codes = new_tile(name + "_codes", [P, width], U32)
+            plane = new_tile(name + "_plane", [P, width], U8)
+            nc.vector.quantize_mx(out=codes[:].bitcast(FP8X4), scales=plane[:], in_=values)
+            return codes, plane
+
+        def product(bank_name, rows, picked):
+            bank = ps.tile([P, PAIR, I], F32, name=bank_name)
+            for r in range(PAIR):
+                cols = slice(r * P, (r + 1) * P)
+                nc.tensor.matmul_mx(out=bank[:, r, :], lhsT=rows[0][:, cols].bitcast(FP8X4), lhsT_scale=rows[1][:, cols],
+                                    rhs=picked[0][:].bitcast(FP4X4), rhs_scale=picked[1][:], start=True, stop=True)
+            return bank
+
+        keys = gather("key", key_words, key_bytes)
+        dealt_query = [deal("query", query_raw, 0, nc.vector.tensor_copy), deal("query", query_raw, 1, nc.scalar.copy)]
+        scores = [product("score_bank%d" % h, quantize("query%d" % h, dealt_query[h]), keys) for h in range(HALVES)]
+        vals = gather("val", val_words, val_bytes)
+
+        page_scale = new_tile("page_scale", [P, PACK], F32)
+        neg_page_scale = new_tile("neg_page_scale", [P, PACK], F32)
+        nc.vector.scalar_tensor_tensor(out=page_scale[:], in0=help_col[:], scalar=1.0 / PAGE, in1=qs_col[:],
+                                       op0=ALU.mult, op1=ALU.mult)
+        nc.vector.scalar_tensor_tensor(out=neg_page_scale[:], in0=help_col[:], scalar=-1.0 / PAGE, in1=qs_col[:],
+                                       op0=ALU.mult, op1=ALU.mult)
+
+        def paged(ap):
+            return ap.rearrange("p r (g j) -> p (r g) j", j=PAGE)
+
+        def per_page(ap):
+            return ap.rearrange("p r g -> p (r g)").unsqueeze(2).to_broadcast([P, PAIR * G, PAGE])
+
+        def halves(name, shape, dtype=F32):
+            return [new_tile("%s%d" % (name, h), shape, dtype) for h in range(HALVES)]
+
+        page_sum = halves("page_sum", [P, PAIR * G])
+        tanh = halves("tanh", [P, PAIR, G])
+        factor = halves("factor", [P, PAIR, G])
+        tanh_sq = halves("tanh_sq", [P, PAIR, G])
+        unnormed = halves("unnormed", [P, PAIR, 2, G])
+        normed = halves("normed", [P, 2, PAIR, G])
+        helped = halves("helped", [P, PAIR, I])
+        neg_max = halves("neg_max", [P, PAIR])
+        prob = halves("prob", [P, PAIR, I])
+        total = halves("total", [P, PAIR])
+        inv_total = halves("inv_total", [P, PAIR])
+        weighted = halves("weighted", [P, PAIR, I])
+        mean = halves("mean", [P, PAIR])
+        centred = halves("centred", [P, PAIR, I])
+        through = halves("through", [P, PAIR, I])
+        through_sum = halves("through_sum", [P, PAIR, G])
+        page_term = halves("page_term", [P, PAIR, G])
+
+        for h in range(HALVES):
+            nc.vector.tensor_reduce(out=page_sum[h][:], in_=paged(scores[h][:]), axis=AX.X, op=ALU.add)
+            nc.scalar.activation(out=tanh[h][:].rearrange("p r g -> p (r g)"), in_=page_sum[h][:], func=ACT.Tanh,
+                                 scale=2.0 / PAGE)
+            for r in range(PAIR):
+                row = PAIR * h + r
+                nc.scalar.activation(out=factor[h][:, r, :], in_=tanh[h][:, r, :], func=ACT.Identity,
+                                     scale=half_help[:, row:row + 1], bias=half_help1[:, row:row + 1])
+
+        dealt_gout = [deal("gout", gout_raw, 0, nc.scalar.copy)]
+
+        for h in range(HALVES):
+            nc.vector.tensor_tensor(out=paged(helped[h][:]), in0=paged(scores[h][:]), in1=per_page(factor[h][:]),
+                                    op=ALU.mult)
+        for h in range(HALVES):
+            nc.vector.tensor_reduce(out=neg_max[h][:], in_=helped[h][:], axis=AX.X, op=ALU.max, negate=True)
+            for r in range(PAIR):
+                nc.scalar.activation(out=prob[h][:, r, :], in_=helped[h][:, r, :], func=ACT.Exp,
+                                     bias=neg_max[h][:, r:r + 1], accum_out=total[h][:, r:r + 1])
+        dealt_gout.append(deal("gout", gout_raw, 1, nc.scalar.copy, tag="helped0"))
+        grads = [product("grad_bank%d" % h, quantize("gout%d" % h, dealt_gout[h]), vals) for h in range(HALVES)]
+
+        for h in range(HALVES):
+            nc.scalar.activation(out=tanh_sq[h][:], in_=tanh[h][:], func=ACT.Square)
+            for r in range(PAIR):
+                row = PAIR * h + r
+                nc.scalar.activation(out=unnormed[h][:, r, 0, :], in_=factor[h][:, r, :], func=ACT.Copy,
+                                     scale=qs_col[:, row:row + 1])
+                nc.scalar.activation(out=unnormed[h][:, r, 1, :], in_=tanh_sq[h][:, r, :], func=ACT.Identity,
+                                     scale=neg_page_scale[:, row:row + 1], bias=page_scale[:, row:row + 1])
+
+        faded = [new_tile("faded%d" % c, [P, U], F32) for c in range(D // P)]
+        for c in range(D // P):
+            for u0 in range(0, U, FADE_COLS):
+                cols = slice(u0, u0 + FADE_COLS)
+                nc.gpsimd.tensor_tensor(out=faded[c][:, cols], in0=olds[c][:, cols], in1=fade_rows[:, cols], op=ALU.mult)
+
+        def invert(h):
+            nc.vector.reciprocal(out=inv_total[h][:], in_=total[h][:])
+            for r in range(PAIR):
+                nc.scalar.activation(out=normed[h][:, :, r, :], in_=unnormed[h][:, r, :, :], func=ACT.Copy,
+                                     scale=inv_total[h][:, r:r + 1])
+
+        def weigh(h, r):
+            nc.vector.scalar_tensor_tensor(out=weighted[h][:, r, :], in0=grads[h][:, r, :], scalar=inv_total[h][:, r:r + 1],
+                                           in1=prob[h][:, r, :], op0=ALU.mult, op1=ALU.mult,
+                                           accum_out=mean[h][:, r:r + 1])
+
+        def centre(h, r):
+            nc.vector.scalar_tensor_tensor(out=centred[h][:, r, :], in0=grads[h][:, r, :], scalar=mean[h][:, r:r + 1],
+                                           in1=prob[h][:, r, :], op0=ALU.subtract, op1=ALU.mult)
+
+        def times_scores(h):
+            nc.vector.tensor_tensor(out=through[h][:], in0=scores[h][:], in1=centred[h][:], op=ALU.mult)
+
+        def sum_pages(h):
+            nc.vector.tensor_reduce(out=through_sum[h][:].rearrange("p r g -> p (r g)"), in_=paged(through[h][:]),
+                                    axis=AX.X, op=ALU.add)
+
+        def make_page_term(h):
+            nc.vector.tensor_tensor(out=page_term[h][:], in0=through_sum[h][:], in1=normed[h][:, 1, :, :], op=ALU.mult)
+
+        gs = new_tile("gs", [P, I, PACK], BF16)
+
+        def finish_on_scalar(h, pages):
+            for g in pages:
+                cols = slice(g * PAGE, (g + 1) * PAGE)
+                for r in range(PAIR):
+                    nc.scalar.activation(out=gs[:, cols, PAIR * h + r], in_=centred[h][:, r, cols], func=ACT.Identity,
+                                         scale=normed[h][:, 0, r, g:g + 1], bias=page_term[h][:, r, g:g + 1])
+
+        rest = G - SCALAR_PAGES
+        rest_cols = slice(SCALAR_PAGES * PAGE, I)
+        scaled = new_tile("scaled", [P, rest, PAGE, PAIR], F32)
+
+        def spread(ap):
+            return ap[:, :, SCALAR_PAGES:].rearrange("p r g -> p g r").unsqueeze(2).to_broadcast([P, rest, PAGE, PAIR])
+
+        woven_tags = ["helped1", "centred0", "qrows0_codes", "qrows1_codes"]
+
+        def weave(c):
+            woven = new_tile("woven%d" % c, [P, P, PACK], BF16, tag=woven_tags[c])
+            nc.scalar.copy(out=woven[:].rearrange("p (c i) r -> p c r i", i=4),
+                           in_=qrows_raw[:, :, c * P:(c + 1) * P].rearrange("p r (c i) -> p c r i", i=4))
+            return woven[:].rearrange("p d r -> p (d r)")
+
+        invert(0)
+        weigh(0, 0)
+        weigh(0, 1)
+        invert(1)
+        centre(0, 0)
+        weigh(1, 0)
+        centre(0, 1)
+        weigh(1, 1)
+        times_scores(0)
+        centre(1, 0)
+        sum_pages(0)
+        centre(1, 1)
+        make_page_term(0)
+        finish_on_scalar(0, range(G))
+        times_scores(1)
+        nc.vector.tensor_tensor(out=scaled[:],
+                                in0=centred[1][:, :, rest_cols].rearrange("p r (g j) -> p g j r", j=PAGE),
+                                in1=spread(normed[1][:, 0, :, :]), op=ALU.mult)
+        sum_pages(1)
+        rows_mx = [quantize("qrows0", weave(0))]
+        make_page_term(1)
+        finish_on_scalar(1, range(SCALAR_PAGES))
+        nc.vector.tensor_tensor(out=gs[:, rest_cols, PAIR:].rearrange("p (g j) r -> p g j r", j=PAGE),
+                                in0=scaled[:], in1=spread(page_term[1][:]), op=ALU.add)
+        gs_mx = quantize("gs", gs[:].rearrange("p i r -> p (i r)"))
+
+        bank_names = ["score_bank0", "grad_bank0", "score_bank1", "grad_bank1"]
+        for c in range(D // P):
+            if c + 1 < D // P:
+                rows_mx.append(quantize("qrows%d" % (c + 1), weave(c + 1)))
+            bank = ps.tile([P, PAIR, I], F32, name=bank_names[c])
+            nc.tensor.matmul_mx(out=bank[:, 0, :], lhsT=rows_mx[c][0][:].bitcast(FP8X4), lhsT_scale=rows_mx[c][1][:],
+                                rhs=gs_mx[0][:].bitcast(FP8X4), rhs_scale=gs_mx[1][:], start=True, stop=True)
+            key_grad = new_tile("key_grad%d" % c, [P, I], F32)
+            nc.scalar.copy(out=key_grad[:], in_=bank[:, 0, :])
+            nc.vector.tensor_copy(windows[c][:].indirect(places[:]), key_grad[:])
+        for c in range(D // P):
+            engine = nc.gpsimd if c < GPSIMD_ADD_TILES else nc.vector
+            result = new_tile("result%d" % c, [P, U], F32)
+            for u0 in range(0, U, U // 2):
+                cols = slice(u0, u0 + U // 2)
+                engine.tensor_tensor(out=result[:, cols], in0=windows[c][:, cols], in1=faded[c][:, cols], op=ALU.add)
+                nc.sync.dma_start(out=out[c * P:(c + 1) * P, cols], in_=result[:, cols])

@@ -23,9 +23,9 @@ PACK = 4
 PAGE = I // G
 HALVES = 2
 PAIR = 2
-SCALAR_PAGES = 0
+SCALAR_PAGES = 4
 FADE_COLS = 256
-GPSIMD_ADD_TILES = 2
+GPSIMD_ADD_TILES = 0
 
 
 def tile_attend_bpagemates_k_kernel(tc, query, keys_words, keys_scales, helpf, gout, vals_words, vals_scales,
@@ -67,12 +67,13 @@ def tile_attend_bpagemates_k_kernel(tc, query, keys_words, keys_scales, helpf, g
         load_bytes(val_bytes, vals_scales)
         fade_col = new_tile("fade_col", [P, U // P], F32)
         nc.sync.dma_start(out=fade_col[:], in_=fade.rearrange("o (n m) -> (o n) m", n=P))
+        olds = [new_tile("old%d" % c, [P, U], F32) for c in range(D // P)]
+        nc.sync.dma_start(out=olds[0][:], in_=old[0:P, :])
         gout_raw = new_tile("gout_raw", [P, PACK, Q], F32)
         nc.sync.dma_start(out=gout_raw[:], in_=gout.rearrange("(p j) q -> p j q", j=PACK))
         qs_col = new_tile("qs_col", [P, PACK], F32)
         nc.sync.dma_start(out=qs_col[:], in_=qs.rearrange("(p r) o -> p (r o)", r=PACK))
-        olds = [new_tile("old%d" % c, [P, U], F32) for c in range(D // P)]
-        for c in range(D // P):
+        for c in range(1, D // P):
             nc.sync.dma_start(out=olds[c][:], in_=old[c * P:(c + 1) * P, :])
         qrows_raw = new_tile("qrows_raw", [P, PACK, D], F32)
         nc.sync.dma_start(out=qrows_raw[:], in_=qrows.rearrange("(p r) d -> p r d", r=PACK))
@@ -223,21 +224,22 @@ def tile_attend_bpagemates_k_kernel(tc, query, keys_words, keys_scales, helpf, g
         def make_page_term(h):
             nc.vector.tensor_tensor(out=page_term[h][:], in0=through_sum[h][:], in1=normed[h][:, 1, :, :], op=ALU.mult)
 
+        planes = new_tile("planes", [P, PACK, I], BF16)
         gs = new_tile("gs", [P, I, PACK], BF16)
 
         def finish_on_scalar(h, pages):
             for g in pages:
                 cols = slice(g * PAGE, (g + 1) * PAGE)
                 for r in range(PAIR):
-                    nc.scalar.activation(out=gs[:, cols, PAIR * h + r], in_=centred[h][:, r, cols], func=ACT.Identity,
+                    nc.scalar.activation(out=planes[:, PAIR * h + r, cols], in_=centred[h][:, r, cols], func=ACT.Identity,
                                          scale=normed[h][:, 0, r, g:g + 1], bias=page_term[h][:, r, g:g + 1])
 
         rest = G - SCALAR_PAGES
         rest_cols = slice(SCALAR_PAGES * PAGE, I)
-        scaled = new_tile("scaled", [P, rest, PAGE, PAIR], F32)
+        scaled = new_tile("scaled", [P, PAIR, rest, PAGE], F32)
 
         def spread(ap):
-            return ap[:, :, SCALAR_PAGES:].rearrange("p r g -> p g r").unsqueeze(2).to_broadcast([P, rest, PAGE, PAIR])
+            return ap[:, :, SCALAR_PAGES:].unsqueeze(3).to_broadcast([P, PAIR, rest, PAGE])
 
         woven_tags = ["helped1", "centred0", "qrows0_codes", "qrows1_codes"]
 
@@ -263,14 +265,16 @@ def tile_attend_bpagemates_k_kernel(tc, query, keys_words, keys_scales, helpf, g
         finish_on_scalar(0, range(G))
         times_scores(1)
         nc.vector.tensor_tensor(out=scaled[:],
-                                in0=centred[1][:, :, rest_cols].rearrange("p r (g j) -> p g j r", j=PAGE),
+                                in0=centred[1][:, :, rest_cols].rearrange("p r (g j) -> p r g j", j=PAGE),
                                 in1=spread(normed[1][:, 0, :, :]), op=ALU.mult)
         sum_pages(1)
         rows_mx = [quantize("qrows0", weave(0))]
         make_page_term(1)
         finish_on_scalar(1, range(SCALAR_PAGES))
-        nc.vector.tensor_tensor(out=gs[:, rest_cols, PAIR:].rearrange("p (g j) r -> p g j r", j=PAGE),
+        nc.vector.tensor_tensor(out=planes[:, PAIR:, rest_cols].rearrange("p r (g j) -> p r g j", j=PAGE),
                                 in0=scaled[:], in1=spread(page_term[1][:]), op=ALU.add)
+        nc.vector.tensor_copy(out=gs[:].rearrange("p (c i) r -> p c r i", i=4),
+                              in_=planes[:].rearrange("p r (c i) -> p c r i", i=4))
         gs_mx = quantize("gs", gs[:].rearrange("p i r -> p (i r)"))
 
         bank_names = ["score_bank0", "grad_bank0", "score_bank1", "grad_bank1"]

@@ -23,9 +23,7 @@ PACK = 4
 PAGE = I // G
 HALVES = 2
 PAIR = 2
-SCALAR_PAGES = 4
-FADE_COLS = 256
-GPSIMD_ADD_TILES = 0
+BLOCKS = U // P
 
 
 def tile_attend_bpagemates_k_kernel(tc, query, keys_words, keys_scales, helpf, gout, vals_words, vals_scales,
@@ -65,35 +63,32 @@ def tile_attend_bpagemates_k_kernel(tc, query, keys_words, keys_scales, helpf, g
         help_col = new_tile("help_col", [P, PACK], F32)
         nc.sync.dma_start(out=help_col[:], in_=helpf.rearrange("(p r) o -> p (r o)", r=PACK))
         load_bytes(val_bytes, vals_scales)
-        fade_col = new_tile("fade_col", [P, U // P], F32)
-        nc.sync.dma_start(out=fade_col[:], in_=fade.rearrange("o (n m) -> (o n) m", n=P))
-        olds = [new_tile("old%d" % c, [P, U], F32) for c in range(D // P)]
-        nc.sync.dma_start(out=olds[0][:], in_=old[0:P, :])
         gout_raw = new_tile("gout_raw", [P, PACK, Q], F32)
         nc.sync.dma_start(out=gout_raw[:], in_=gout.rearrange("(p j) q -> p j q", j=PACK))
         qs_col = new_tile("qs_col", [P, PACK], F32)
         nc.sync.dma_start(out=qs_col[:], in_=qs.rearrange("(p r) o -> p (r o)", r=PACK))
-        for c in range(1, D // P):
-            nc.sync.dma_start(out=olds[c][:], in_=old[c * P:(c + 1) * P, :])
+        fade_rows = new_tile("fade_rows", [P, P], F32)
+        nc.sync.dma_start(out=fade_rows[:],
+                          in_=fade.rearrange("o (m n) -> (o m) n", n=P).unsqueeze(0).to_broadcast([P // BLOCKS, BLOCKS, P]))
         qrows_raw = new_tile("qrows_raw", [P, PACK, D], F32)
         nc.sync.dma_start(out=qrows_raw[:], in_=qrows.rearrange("(p r) d -> p r d", r=PACK))
+        olds = [new_tile("old%d" % c, [P, U], F32) for c in range(D // P)]
+        for c in range(D // P):
+            nc.sync.dma_start(out=olds[c][:], in_=old[c * P:(c + 1) * P, :])
         nc.sync.dma_start(places[:], offs4)
 
         half_help = new_tile("half_help", [P, PACK], F32, tag="gout_dealt0")
-        half_help1 = new_tile("half_help1", [P, PACK], F32)
+        half_help1 = new_tile("half_help1", [P, PACK], F32, tag="gout_dealt1")
         nc.scalar.activation(out=half_help[:], in_=help_col[:], func=ACT.Copy, scale=0.5)
         nc.scalar.activation(out=half_help1[:], in_=help_col[:], func=ACT.Copy, scale=0.5, bias=1.0)
 
+        page_help = new_tile("page_help", [P, PACK], F32)
+        neg_page_help = new_tile("neg_page_help", [P, PACK], F32)
+        nc.scalar.activation(out=page_help[:], in_=help_col[:], func=ACT.Copy, scale=1.0 / PAGE)
+        nc.scalar.activation(out=neg_page_help[:], in_=help_col[:], func=ACT.Copy, scale=-1.0 / PAGE)
+
         ident = new_tile("ident", [P, P], F32)
         make_identity(nc, ident[:])
-        fade_rows = new_tile("fade_rows", [P, U], F32)
-        for b in range(2):
-            bank = ps.tile([P, 4, P], F32, name="fade_bank%d" % b)
-            for m in range(4):
-                col = 4 * b + m
-                nc.tensor.transpose(bank[:, m, :], fade_col[:, col:col + 1].to_broadcast([P, P]), ident[:])
-            nc.scalar.copy(out=fade_rows[:].rearrange("p (n m) -> p n m", n=P)[:, :, 4 * b:4 * b + 4],
-                           in_=bank[:].rearrange("p m n -> p n m"))
 
         def gather(name, words, plane):
             picked_words = new_tile(name + "_picked_words", [P, I], U16)
@@ -128,13 +123,6 @@ def tile_attend_bpagemates_k_kernel(tc, query, keys_words, keys_scales, helpf, g
         scores = [product("score_bank%d" % h, quantize("query%d" % h, dealt_query[h]), keys) for h in range(HALVES)]
         vals = gather("val", val_words, val_bytes)
 
-        page_scale = new_tile("page_scale", [P, PACK], F32)
-        neg_page_scale = new_tile("neg_page_scale", [P, PACK], F32)
-        nc.vector.scalar_tensor_tensor(out=page_scale[:], in0=help_col[:], scalar=1.0 / PAGE, in1=qs_col[:],
-                                       op0=ALU.mult, op1=ALU.mult)
-        nc.vector.scalar_tensor_tensor(out=neg_page_scale[:], in0=help_col[:], scalar=-1.0 / PAGE, in1=qs_col[:],
-                                       op0=ALU.mult, op1=ALU.mult)
-
         def paged(ap):
             return ap.rearrange("p r (g j) -> p (r g) j", j=PAGE)
 
@@ -146,12 +134,12 @@ def tile_attend_bpagemates_k_kernel(tc, query, keys_words, keys_scales, helpf, g
 
         page_sum = halves("page_sum", [P, PAIR * G])
         tanh = halves("tanh", [P, PAIR, G])
-        factor = halves("factor", [P, PAIR, G])
-        tanh_sq = halves("tanh_sq", [P, PAIR, G])
-        unnormed = halves("unnormed", [P, PAIR, 2, G])
+        coeff = halves("coeff", [P, 2, PAIR, G])
+        unnormed = halves("unnormed", [P, 2, PAIR, G])
         normed = halves("normed", [P, 2, PAIR, G])
         helped = halves("helped", [P, PAIR, I])
         neg_max = halves("neg_max", [P, PAIR])
+        tanh_sq = [new_tile("tanh_sq%d" % h, [P, PAIR, G], F32, tag="neg_max%d" % h) for h in range(HALVES)]
         prob = halves("prob", [P, PAIR, I])
         total = halves("total", [P, PAIR])
         inv_total = halves("inv_total", [P, PAIR])
@@ -168,41 +156,34 @@ def tile_attend_bpagemates_k_kernel(tc, query, keys_words, keys_scales, helpf, g
                                  scale=2.0 / PAGE)
             for r in range(PAIR):
                 row = PAIR * h + r
-                nc.scalar.activation(out=factor[h][:, r, :], in_=tanh[h][:, r, :], func=ACT.Identity,
+                nc.scalar.activation(out=coeff[h][:, 0, r, :], in_=tanh[h][:, r, :], func=ACT.Identity,
                                      scale=half_help[:, row:row + 1], bias=half_help1[:, row:row + 1])
 
-        dealt_gout = [deal("gout", gout_raw, 0, nc.scalar.copy)]
+        dealt_gout = [deal("gout", gout_raw, h, nc.scalar.copy) for h in range(HALVES)]
 
         for h in range(HALVES):
-            nc.vector.tensor_tensor(out=paged(helped[h][:]), in0=paged(scores[h][:]), in1=per_page(factor[h][:]),
+            nc.vector.tensor_tensor(out=paged(helped[h][:]), in0=paged(scores[h][:]), in1=per_page(coeff[h][:, 0, :, :]),
                                     op=ALU.mult)
         for h in range(HALVES):
             nc.vector.tensor_reduce(out=neg_max[h][:], in_=helped[h][:], axis=AX.X, op=ALU.max, negate=True)
             for r in range(PAIR):
                 nc.scalar.activation(out=prob[h][:, r, :], in_=helped[h][:, r, :], func=ACT.Exp,
                                      bias=neg_max[h][:, r:r + 1], accum_out=total[h][:, r:r + 1])
-        dealt_gout.append(deal("gout", gout_raw, 1, nc.scalar.copy, tag="helped0"))
         grads = [product("grad_bank%d" % h, quantize("gout%d" % h, dealt_gout[h]), vals) for h in range(HALVES)]
 
         for h in range(HALVES):
             nc.scalar.activation(out=tanh_sq[h][:], in_=tanh[h][:], func=ACT.Square)
             for r in range(PAIR):
                 row = PAIR * h + r
-                nc.scalar.activation(out=unnormed[h][:, r, 0, :], in_=factor[h][:, r, :], func=ACT.Copy,
+                nc.scalar.activation(out=coeff[h][:, 1, r, :], in_=tanh_sq[h][:, r, :], func=ACT.Identity,
+                                     scale=neg_page_help[:, row:row + 1], bias=page_help[:, row:row + 1])
+                nc.scalar.activation(out=unnormed[h][:, :, r, :], in_=coeff[h][:, :, r, :], func=ACT.Copy,
                                      scale=qs_col[:, row:row + 1])
-                nc.scalar.activation(out=unnormed[h][:, r, 1, :], in_=tanh_sq[h][:, r, :], func=ACT.Identity,
-                                     scale=neg_page_scale[:, row:row + 1], bias=page_scale[:, row:row + 1])
-
-        faded = [new_tile("faded%d" % c, [P, U], F32) for c in range(D // P)]
-        for c in range(D // P):
-            for u0 in range(0, U, FADE_COLS):
-                cols = slice(u0, u0 + FADE_COLS)
-                nc.gpsimd.tensor_tensor(out=faded[c][:, cols], in0=olds[c][:, cols], in1=fade_rows[:, cols], op=ALU.mult)
 
         def invert(h):
             nc.vector.reciprocal(out=inv_total[h][:], in_=total[h][:])
             for r in range(PAIR):
-                nc.scalar.activation(out=normed[h][:, :, r, :], in_=unnormed[h][:, r, :, :], func=ACT.Copy,
+                nc.scalar.activation(out=normed[h][:, :, r, :], in_=unnormed[h][:, :, r, :], func=ACT.Copy,
                                      scale=inv_total[h][:, r:r + 1])
 
         def weigh(h, r):
@@ -224,30 +205,39 @@ def tile_attend_bpagemates_k_kernel(tc, query, keys_words, keys_scales, helpf, g
         def make_page_term(h):
             nc.vector.tensor_tensor(out=page_term[h][:], in0=through_sum[h][:], in1=normed[h][:, 1, :, :], op=ALU.mult)
 
-        planes = new_tile("planes", [P, PACK, I], BF16)
-        gs = new_tile("gs", [P, I, PACK], BF16)
+        planes = halves("planes", [P, PACK, I // 2], BF16)
 
-        def finish_on_scalar(h, pages):
-            for g in pages:
-                cols = slice(g * PAGE, (g + 1) * PAGE)
+        def finish_on_scalar(h, part):
+            for g in range(part * G // 2, (part + 1) * G // 2):
+                local = slice(g * PAGE - part * I // 2, (g + 1) * PAGE - part * I // 2)
                 for r in range(PAIR):
-                    nc.scalar.activation(out=planes[:, PAIR * h + r, cols], in_=centred[h][:, r, cols], func=ACT.Identity,
+                    nc.scalar.activation(out=planes[part][:, PAIR * h + r, local],
+                                         in_=centred[h][:, r, g * PAGE:(g + 1) * PAGE], func=ACT.Identity,
                                          scale=normed[h][:, 0, r, g:g + 1], bias=page_term[h][:, r, g:g + 1])
 
-        rest = G - SCALAR_PAGES
-        rest_cols = slice(SCALAR_PAGES * PAGE, I)
-        scaled = new_tile("scaled", [P, PAIR, rest, PAGE], F32)
+        scaled = new_tile("scaled", [P, PAIR, G // 2, PAGE], F32)
 
         def spread(ap):
-            return ap[:, :, SCALAR_PAGES:].unsqueeze(3).to_broadcast([P, PAIR, rest, PAGE])
+            return ap[:, :, :G // 2].unsqueeze(3).to_broadcast([P, PAIR, G // 2, PAGE])
 
-        woven_tags = ["helped1", "centred0", "qrows0_codes", "qrows1_codes"]
+        gs_codes = new_tile("gs_codes", [P, I], U32)
+        gs_plane = new_tile("gs_plane", [P, I], U8)
+
+        def quantize_gs(part, copy):
+            gs = new_tile("gs%d" % part, [P, I // 2, PACK], BF16)
+            copy(out=gs[:].rearrange("p (c i) r -> p c r i", i=4),
+                 in_=planes[part][:].rearrange("p r (c i) -> p c r i", i=4))
+            cols = slice(part * I // 2, (part + 1) * I // 2)
+            nc.vector.quantize_mx(out=gs_codes[:, cols].bitcast(FP8X4), scales=gs_plane[:, cols],
+                                  in_=gs[:].rearrange("p i r -> p (i r)"))
+
+        woven = new_tile("woven", [P, D, PACK], BF16, tag="gout_dealt1")
 
         def weave(c):
-            woven = new_tile("woven%d" % c, [P, P, PACK], BF16, tag=woven_tags[c])
-            nc.scalar.copy(out=woven[:].rearrange("p (c i) r -> p c r i", i=4),
-                           in_=qrows_raw[:, :, c * P:(c + 1) * P].rearrange("p r (c i) -> p c r i", i=4))
-            return woven[:].rearrange("p d r -> p (d r)")
+            cols = slice(c * P, (c + 1) * P)
+            nc.gpsimd.tensor_scalar(out=woven[:, cols, :], in0=qrows_raw[:, :, cols].rearrange("p r d -> p d r"),
+                                    scalar1=1.0, scalar2=0.0, op0=ALU.mult, op1=ALU.add)
+            return woven[:, cols, :].rearrange("p d r -> p (d r)")
 
         invert(0)
         weigh(0, 0)
@@ -262,35 +252,102 @@ def tile_attend_bpagemates_k_kernel(tc, query, keys_words, keys_scales, helpf, g
         sum_pages(0)
         centre(1, 1)
         make_page_term(0)
-        finish_on_scalar(0, range(G))
+        finish_on_scalar(0, 0)
+        finish_on_scalar(0, 1)
         times_scores(1)
         nc.vector.tensor_tensor(out=scaled[:],
-                                in0=centred[1][:, :, rest_cols].rearrange("p r (g j) -> p r g j", j=PAGE),
+                                in0=centred[1][:, :, :I // 2].rearrange("p r (g j) -> p r g j", j=PAGE),
                                 in1=spread(normed[1][:, 0, :, :]), op=ALU.mult)
         sum_pages(1)
-        rows_mx = [quantize("qrows0", weave(0))]
+        rows_mx = [quantize("qrows%d" % c, weave(c)) for c in range(2)]
         make_page_term(1)
-        finish_on_scalar(1, range(SCALAR_PAGES))
-        nc.vector.tensor_tensor(out=planes[:, PAIR:, rest_cols].rearrange("p r (g j) -> p r g j", j=PAGE),
+        finish_on_scalar(1, 1)
+        nc.vector.tensor_tensor(out=planes[0][:, PAIR:, :].rearrange("p r (g j) -> p r g j", j=PAGE),
                                 in0=scaled[:], in1=spread(page_term[1][:]), op=ALU.add)
-        nc.vector.tensor_copy(out=gs[:].rearrange("p (c i) r -> p c r i", i=4),
-                              in_=planes[:].rearrange("p r (c i) -> p c r i", i=4))
-        gs_mx = quantize("gs", gs[:].rearrange("p i r -> p (i r)"))
+        quantize_gs(0, nc.vector.tensor_copy)
+        quantize_gs(1, nc.scalar.copy)
+        rows_mx.extend(quantize("qrows%d" % c, weave(c)) for c in range(2, D // P))
 
-        bank_names = ["score_bank0", "grad_bank0", "score_bank1", "grad_bank1"]
-        for c in range(D // P):
-            if c + 1 < D // P:
-                rows_mx.append(quantize("qrows%d" % (c + 1), weave(c + 1)))
-            bank = ps.tile([P, PAIR, I], F32, name=bank_names[c])
-            nc.tensor.matmul_mx(out=bank[:, 0, :], lhsT=rows_mx[c][0][:].bitcast(FP8X4), lhsT_scale=rows_mx[c][1][:],
-                                rhs=gs_mx[0][:].bitcast(FP8X4), rhs_scale=gs_mx[1][:], start=True, stop=True)
-            key_grad = new_tile("key_grad%d" % c, [P, I], F32)
-            nc.scalar.copy(out=key_grad[:], in_=bank[:, 0, :])
-            nc.vector.tensor_copy(windows[c][:].indirect(places[:]), key_grad[:])
-        for c in range(D // P):
-            engine = nc.gpsimd if c < GPSIMD_ADD_TILES else nc.vector
-            result = new_tile("result%d" % c, [P, U], F32)
-            for u0 in range(0, U, U // 2):
-                cols = slice(u0, u0 + U // 2)
-                engine.tensor_tensor(out=result[:, cols], in0=windows[c][:, cols], in1=faded[c][:, cols], op=ALU.add)
-                nc.sync.dma_start(out=out[c * P:(c + 1) * P, cols], in_=result[:, cols])
+        def scatter_key_grad(c, first, count, bank_name):
+            cols = slice(first, first + count)
+            bank = ps.tile([P, count], F32, name=bank_name)
+            nc.tensor.matmul_mx(out=bank[:], lhsT=rows_mx[c][0][:].bitcast(FP8X4), lhsT_scale=rows_mx[c][1][:],
+                                rhs=gs_codes[:, cols].bitcast(FP8X4), rhs_scale=gs_plane[:, cols], start=True, stop=True)
+            key_grad = new_tile("key_grad%d_%d" % (c, first), [P, count], F32)
+            nc.scalar.copy(out=key_grad[:], in_=bank[:])
+            nc.vector.tensor_copy(windows[c][:].indirect(places[:, first // 16:(first + count) // 16]), key_grad[:])
+
+        scatter_key_grad(0, 0, I // 2, "score_bank0")
+        scatter_key_grad(0, I // 2, I // 2, "grad_bank1")
+        scatter_key_grad(1, 0, I, "score_bank1")
+        scatter_key_grad(2, 0, I, "grad_bank0")
+        scatter_key_grad(3, 0, I, "score_bank0")
+
+        fade_bank = ps.tile([P, 2, PAIR, P], F32, name="turn_bank3")
+        nc.tensor.transpose(fade_bank[:, 0, 0, :], fade_rows[:], ident[:])
+        fade_col = new_tile("fade_col", [P, BLOCKS], F32)
+        nc.scalar.copy(out=fade_col[:], in_=fade_bank[:, 0, 0, 0:BLOCKS])
+
+        holds = [["helped1", "qrows0_plane"], ["qrows0_codes", None]]
+        faded = [[new_tile("faded%d_%d" % (pair, half), [P, 4, PAIR, P], F32, tag=holds[pair][half]) for half in range(2)]
+                 for pair in range(2)]
+        results = [new_tile("result%d" % c, [P, U], F32) for c in range(D // P)]
+
+        def fade_half(pair, half, bank_names):
+            for n in range(2):
+                m0 = 4 * half + 2 * n
+                bank = ps.tile([P, 2, PAIR, P], F32, name=bank_names[n])
+                for a in range(2):
+                    for b in range(PAIR):
+                        nc.tensor.transpose(bank[:, a, b, :], olds[PAIR * pair + b][:, (m0 + a) * P:(m0 + a + 1) * P], ident[:])
+                for a in range(2):
+                    nc.scalar.activation(out=faded[pair][half][:, 2 * n + a, :, :], in_=bank[:, a, :, :], func=ACT.Copy,
+                                         scale=fade_col[:, m0 + a:m0 + a + 1])
+
+        def store(queue, c, cols):
+            queue.dma_start(out=out[c * P:(c + 1) * P, cols], in_=results[c][:, cols])
+
+        def add_on_vector(c, half, bank_name):
+            bank = ps.tile([P, 4, P], F32, name=bank_name)
+            for a in range(4):
+                nc.tensor.transpose(bank[:, a, :], faded[c // PAIR][half][:, a, c % PAIR, :], ident[:])
+            cols = slice(half * U // 2, (half + 1) * U // 2)
+            nc.vector.tensor_tensor(out=results[c][:, cols], in0=bank[:].rearrange("p a n -> p (a n)"),
+                                    in1=windows[c][:, cols], op=ALU.add)
+            store(nc.sync, c, cols)
+
+        def turn_window(c, bank_names):
+            turned = new_tile("turned%d" % c, [P, BLOCKS, P], F32)
+            for half in range(2):
+                bank = ps.tile([P, 4, P], F32, name=bank_names[half])
+                for a in range(4):
+                    m = 4 * half + a
+                    nc.tensor.transpose(bank[:, a, :], windows[c][:, m * P:(m + 1) * P], ident[:])
+                nc.scalar.copy(out=turned[:, 4 * half:4 * half + 4, :], in_=bank[:])
+            return turned
+
+        def add_in_psum(c, turned, bank_names):
+            for half in range(2):
+                bank = ps.tile([P, 4, P], F32, name=bank_names[half])
+                for a in range(4):
+                    m = 4 * half + a
+                    nc.tensor.matmul(bank[:, a, :], faded[c // PAIR][half][:, a, c % PAIR, :], ident[:], is_transpose=True,
+                                     start=True, stop=False)
+                    nc.tensor.matmul(bank[:, a, :], turned[:, m, :], ident[:], is_transpose=True, start=False, stop=True)
+                cols = slice(half * U // 2, (half + 1) * U // 2)
+                nc.scalar.copy(out=results[c][:, cols], in_=bank[:].rearrange("p a n -> p (a n)"))
+                store(nc.scalar, c, cols)
+
+        turn = ["turn_bank%d" % n for n in range(4)]
+        fade_half(0, 0, turn[:2])
+        fade_half(0, 1, turn[2:])
+        fade_half(1, 0, turn[:2])
+        turned0 = turn_window(0, turn[:2])
+        fade_half(1, 1, turn[2:])
+        add_in_psum(0, turned0, ["grad_bank0", "score_bank0"])
+        add_on_vector(1, 0, "grad_bank1")
+        add_on_vector(1, 1, "score_bank1")
+        add_on_vector(2, 0, turn[2])
+        add_on_vector(3, 0, turn[3])
+        add_on_vector(2, 1, turn[0])
+        add_on_vector(3, 1, turn[1])

from contextlib import ExitStack

import concourse.mybir as mybir
from concourse.masks import make_identity

D, E, T, I, Q, G, U = 512, 512, 1024, 256, 512, 16, 1024
FLOPS = 3 * 2 * 512 * 512 * 256

F32 = mybir.dt.float32
BF16 = mybir.dt.bfloat16
I32 = mybir.dt.int32
U32 = mybir.dt.uint32
U16 = mybir.dt.uint16
U8 = mybir.dt.uint8
FP8X4 = mybir.dt.float8_e4m3fn_x4
FP4X4 = mybir.dt.float4_e2m1fn_x4
ALU = mybir.AluOpType
ACT = mybir.ActivationFunctionType
AX = mybir.AxisListType

P = 128
PACK = 4
PAGE = I // G
HALVES = 2
PAIR = 2
BLOCKS = U // P


def tile_attend_bpagemates_k_kernel(tc, query, keys_words, keys_scales, helpf, gout, vals_words, vals_scales,
                                     qs, qrows, old, fade, offs, offs4, out):
    nc = tc.nc
    with ExitStack() as ctx:
        lists = ctx.enter_context(tc.tile_pool(name="lists", bufs=1))
        sb = ctx.enter_context(tc.tile_pool(name="sb", bufs=1))
        ps = ctx.enter_context(tc.psum_pool(name="ps", bufs=1))

        def new_tile(name, shape, dtype, tag=None):
            return sb.tile(shape, dtype, name=name, tag=tag or name, align_bytes=64)

        slots = lists.tile([P, I // 16], U16, name="slots")
        places = lists.tile([P, I // 16], U16, name="places")

        key_bytes = new_tile("key_bytes", [P, T], U8)
        val_bytes = new_tile("val_bytes", [P, T], U8)
        windows = [new_tile("window%d" % c, [P, U], F32) for c in range(D // P)]
        for window in windows:
            nc.vector.memset(window[:], 0.0)

        def load_bytes(plane, scales):
            for quad in range(4):
                rows = scales[0, 4 * quad:4 * quad + 4, :].bitcast(I32)
                nc.sync.dma_start(out=plane[32 * quad:32 * quad + 32, :].bitcast(I32),
                                  in_=rows.unsqueeze(0).to_broadcast([8, 4, T // 4]))

        nc.sync.dma_start(slots[:], offs)
        key_words = new_tile("key_words", [P, T], U16)
        nc.sync.dma_start(out=key_words[:].bitcast(I32), in_=keys_words[0].bitcast(I32))
        load_bytes(key_bytes, keys_scales)
        val_words = new_tile("val_words", [P, T], U16)
        nc.sync.dma_start(out=val_words[:].bitcast(I32), in_=vals_words[0].bitcast(I32))
        query_raw = new_tile("query_raw", [P, PACK, Q], F32)
        nc.sync.dma_start(out=query_raw[:], in_=query.rearrange("(p j) q -> p j q", j=PACK))
        help_col = new_tile("help_col", [P, PACK], F32)
        nc.sync.dma_start(out=help_col[:], in_=helpf.rearrange("(p r) o -> p (r o)", r=PACK))
        load_bytes(val_bytes, vals_scales)
        gout_raw = new_tile("gout_raw", [P, PACK, Q], F32)
        nc.sync.dma_start(out=gout_raw[:], in_=gout.rearrange("(p j) q -> p j q", j=PACK))
        qs_col = new_tile("qs_col", [P, PACK], F32)
        nc.sync.dma_start(out=qs_col[:], in_=qs.rearrange("(p r) o -> p (r o)", r=PACK))
        fade_rows = new_tile("fade_rows", [P, P], F32)
        nc.sync.dma_start(out=fade_rows[:],
                          in_=fade.rearrange("o (m n) -> (o m) n", n=P).unsqueeze(0).to_broadcast([P // BLOCKS, BLOCKS, P]))
        qrows_raw = new_tile("qrows_raw", [P, PACK, D], F32)
        nc.sync.dma_start(out=qrows_raw[:], in_=qrows.rearrange("(p r) d -> p r d", r=PACK))
        olds = [new_tile("old%d" % c, [P, U], F32) for c in range(D // P)]
        for c in range(D // P):
            nc.sync.dma_start(out=olds[c][:], in_=old[c * P:(c + 1) * P, :])
        nc.sync.dma_start(places[:], offs4)

        half_help = new_tile("half_help", [P, PACK], F32, tag="gout_dealt0")
        half_help1 = new_tile("half_help1", [P, PACK], F32, tag="gout_dealt1")
        nc.scalar.activation(out=half_help[:], in_=help_col[:], func=ACT.Copy, scale=0.5)
        nc.scalar.activation(out=half_help1[:], in_=help_col[:], func=ACT.Copy, scale=0.5, bias=1.0)

        page_help = new_tile("page_help", [P, PACK], F32)
        neg_page_help = new_tile("neg_page_help", [P, PACK], F32)
        nc.scalar.activation(out=page_help[:], in_=help_col[:], func=ACT.Copy, scale=1.0 / PAGE)
        nc.scalar.activation(out=neg_page_help[:], in_=help_col[:], func=ACT.Copy, scale=-1.0 / PAGE)

        ident = new_tile("ident", [P, P], F32)
        make_identity(nc, ident[:])

        def gather(name, words, plane):
            picked_words = new_tile(name + "_picked_words", [P, I], U16)
            picked_bytes = new_tile(name + "_picked_bytes", [P, I], U8)
            nc.vector.tensor_copy(picked_words[:], words[:].indirect(slots[:]))
            nc.vector.tensor_copy(picked_bytes[:], plane[:].indirect(slots[:]))
            return picked_words, picked_bytes

        def deal(name, raw, half, copy, tag=None):
            dealt = new_tile("%s_dealt%d" % (name, half), [P, PAIR, P, PACK], BF16, tag=tag)
            rows = raw[:].rearrange("p j (s r) -> p s j r", r=PACK)[:, :, :, PAIR * half:PAIR * (half + 1)]
            copy(out=dealt[:].rearrange("p r s j -> p s j r"), in_=rows)
            return dealt[:].rearrange("p r s j -> p (r s j)")

        def quantize(name, values):
            width = values.shape[1] // PACK
            codes = new_tile(name + "_codes", [P, width], U32)
            plane = new_tile(name + "_plane", [P, width], U8)
            nc.vector.quantize_mx(out=codes[:].bitcast(FP8X4), scales=plane[:], in_=values)
            return codes, plane

        def product(bank_name, rows, picked):
            bank = ps.tile([P, PAIR, I], F32, name=bank_name)
            for r in range(PAIR):
                cols = slice(r * P, (r + 1) * P)
                nc.tensor.matmul_mx(out=bank[:, r, :], lhsT=rows[0][:, cols].bitcast(FP8X4), lhsT_scale=rows[1][:, cols],
                                    rhs=picked[0][:].bitcast(FP4X4), rhs_scale=picked[1][:], start=True, stop=True)
            return bank

        keys = gather("key", key_words, key_bytes)
        dealt_query = [deal("query", query_raw, 0, nc.vector.tensor_copy), deal("query", query_raw, 1, nc.scalar.copy)]
        scores = [product("score_bank%d" % h, quantize("query%d" % h, dealt_query[h]), keys) for h in range(HALVES)]
        vals = gather("val", val_words, val_bytes)

        def paged(ap):
            return ap.rearrange("p r (g j) -> p (r g) j", j=PAGE)

        def per_page(ap):
            return ap.rearrange("p r g -> p (r g)").unsqueeze(2).to_broadcast([P, PAIR * G, PAGE])

        def halves(name, shape, dtype=F32):
            return [new_tile("%s%d" % (name, h), shape, dtype) for h in range(HALVES)]

        page_sum = halves("page_sum", [P, PAIR * G])
        tanh = halves("tanh", [P, PAIR, G])
        coeff = halves("coeff", [P, 2, PAIR, G])
        unnormed = halves("unnormed", [P, 2, PAIR, G])
        normed = halves("normed", [P, 2, PAIR, G])
        helped = halves("helped", [P, PAIR, I])
        neg_max = halves("neg_max", [P, PAIR])
        tanh_sq = [new_tile("tanh_sq%d" % h, [P, PAIR, G], F32, tag="neg_max%d" % h) for h in range(HALVES)]
        prob = halves("prob", [P, PAIR, I])
        total = halves("total", [P, PAIR])
        inv_total = halves("inv_total", [P, PAIR])
        weighted = halves("weighted", [P, PAIR, I])
        mean = halves("mean", [P, PAIR])
        centred = halves("centred", [P, PAIR, I])
        through = halves("through", [P, PAIR, I])
        through_sum = halves("through_sum", [P, PAIR, G])
        page_term = halves("page_term", [P, PAIR, G])

        for h in range(HALVES):
            nc.vector.tensor_reduce(out=page_sum[h][:], in_=paged(scores[h][:]), axis=AX.X, op=ALU.add)
            nc.scalar.activation(out=tanh[h][:].rearrange("p r g -> p (r g)"), in_=page_sum[h][:], func=ACT.Tanh,
                                 scale=2.0 / PAGE)
            for r in range(PAIR):
                row = PAIR * h + r
                nc.scalar.activation(out=coeff[h][:, 0, r, :], in_=tanh[h][:, r, :], func=ACT.Identity,
                                     scale=half_help[:, row:row + 1], bias=half_help1[:, row:row + 1])

        dealt_gout = [deal("gout", gout_raw, h, nc.scalar.copy) for h in range(HALVES)]

        for h in range(HALVES):
            nc.vector.tensor_tensor(out=paged(helped[h][:]), in0=paged(scores[h][:]), in1=per_page(coeff[h][:, 0, :, :]),
                                    op=ALU.mult)
        for h in range(HALVES):
            nc.vector.tensor_reduce(out=neg_max[h][:], in_=helped[h][:], axis=AX.X, op=ALU.max, negate=True)
            for r in range(PAIR):
                nc.scalar.activation(out=prob[h][:, r, :], in_=helped[h][:, r, :], func=ACT.Exp,
                                     bias=neg_max[h][:, r:r + 1], accum_out=total[h][:, r:r + 1])
        grads = [product("grad_bank%d" % h, quantize("gout%d" % h, dealt_gout[h]), vals) for h in range(HALVES)]

        for h in range(HALVES):
            nc.scalar.activation(out=tanh_sq[h][:], in_=tanh[h][:], func=ACT.Square)
            for r in range(PAIR):
                row = PAIR * h + r
                nc.scalar.activation(out=coeff[h][:, 1, r, :], in_=tanh_sq[h][:, r, :], func=ACT.Identity,
                                     scale=neg_page_help[:, row:row + 1], bias=page_help[:, row:row + 1])
                nc.scalar.activation(out=unnormed[h][:, :, r, :], in_=coeff[h][:, :, r, :], func=ACT.Copy,
                                     scale=qs_col[:, row:row + 1])

        def invert(h):
            nc.vector.reciprocal(out=inv_total[h][:], in_=total[h][:])
            for r in range(PAIR):
                nc.scalar.activation(out=normed[h][:, :, r, :], in_=unnormed[h][:, :, r, :], func=ACT.Copy,
                                     scale=inv_total[h][:, r:r + 1])

        def weigh(h, r):
            nc.vector.scalar_tensor_tensor(out=weighted[h][:, r, :], in0=grads[h][:, r, :], scalar=inv_total[h][:, r:r + 1],
                                           in1=prob[h][:, r, :], op0=ALU.mult, op1=ALU.mult,
                                           accum_out=mean[h][:, r:r + 1])

        def centre(h, r):
            nc.vector.scalar_tensor_tensor(out=centred[h][:, r, :], in0=grads[h][:, r, :], scalar=mean[h][:, r:r + 1],
                                           in1=prob[h][:, r, :], op0=ALU.subtract, op1=ALU.mult)

        def times_scores(h):
            nc.vector.tensor_tensor(out=through[h][:], in0=scores[h][:], in1=centred[h][:], op=ALU.mult)

        def sum_pages(h):
            nc.vector.tensor_reduce(out=through_sum[h][:].rearrange("p r g -> p (r g)"), in_=paged(through[h][:]),
                                    axis=AX.X, op=ALU.add)

        def make_page_term(h):
            nc.vector.tensor_tensor(out=page_term[h][:], in0=through_sum[h][:], in1=normed[h][:, 1, :, :], op=ALU.mult)

        planes = halves("planes", [P, PACK, I // 2], BF16)

        def finish_on_scalar(h, part):
            for g in range(part * G // 2, (part + 1) * G // 2):
                local = slice(g * PAGE - part * I // 2, (g + 1) * PAGE - part * I // 2)
                for r in range(PAIR):
                    nc.scalar.activation(out=planes[part][:, PAIR * h + r, local],
                                         in_=centred[h][:, r, g * PAGE:(g + 1) * PAGE], func=ACT.Identity,
                                         scale=normed[h][:, 0, r, g:g + 1], bias=page_term[h][:, r, g:g + 1])

        scaled = new_tile("scaled", [P, PAIR, G // 2, PAGE], F32)

        def spread(ap):
            return ap[:, :, :G // 2].unsqueeze(3).to_broadcast([P, PAIR, G // 2, PAGE])

        gs_codes = new_tile("gs_codes", [P, I], U32)
        gs_plane = new_tile("gs_plane", [P, I], U8)

        def quantize_gs(part, copy):
            gs = new_tile("gs%d" % part, [P, I // 2, PACK], BF16)
            copy(out=gs[:].rearrange("p (c i) r -> p c r i", i=4),
                 in_=planes[part][:].rearrange("p r (c i) -> p c r i", i=4))
            cols = slice(part * I // 2, (part + 1) * I // 2)
            nc.vector.quantize_mx(out=gs_codes[:, cols].bitcast(FP8X4), scales=gs_plane[:, cols],
                                  in_=gs[:].rearrange("p i r -> p (i r)"))

        woven = new_tile("woven", [P, D, PACK], BF16, tag="gout_dealt1")

        def weave(c):
            cols = slice(c * P, (c + 1) * P)
            nc.gpsimd.tensor_scalar(out=woven[:, cols, :], in0=qrows_raw[:, :, cols].rearrange("p r d -> p d r"),
                                    scalar1=1.0, scalar2=0.0, op0=ALU.mult, op1=ALU.add)
            return woven[:, cols, :].rearrange("p d r -> p (d r)")

        invert(0)
        weigh(0, 0)
        weigh(0, 1)
        invert(1)
        centre(0, 0)
        weigh(1, 0)
        centre(0, 1)
        weigh(1, 1)
        times_scores(0)
        centre(1, 0)
        sum_pages(0)
        centre(1, 1)
        make_page_term(0)
        finish_on_scalar(0, 0)
        finish_on_scalar(0, 1)
        times_scores(1)
        nc.vector.tensor_tensor(out=scaled[:],
                                in0=centred[1][:, :, :I // 2].rearrange("p r (g j) -> p r g j", j=PAGE),
                                in1=spread(normed[1][:, 0, :, :]), op=ALU.mult)
        sum_pages(1)
        rows_mx = [quantize("qrows%d" % c, weave(c)) for c in range(2)]
        make_page_term(1)
        finish_on_scalar(1, 1)
        nc.vector.tensor_tensor(out=planes[0][:, PAIR:, :].rearrange("p r (g j) -> p r g j", j=PAGE),
                                in0=scaled[:], in1=spread(page_term[1][:]), op=ALU.add)
        quantize_gs(0, nc.vector.tensor_copy)
        quantize_gs(1, nc.scalar.copy)
        rows_mx.extend(quantize("qrows%d" % c, weave(c)) for c in range(2, D // P))

        def scatter_key_grad(c, first, count, bank_name):
            cols = slice(first, first + count)
            bank = ps.tile([P, count], F32, name=bank_name)
            nc.tensor.matmul_mx(out=bank[:], lhsT=rows_mx[c][0][:].bitcast(FP8X4), lhsT_scale=rows_mx[c][1][:],
                                rhs=gs_codes[:, cols].bitcast(FP8X4), rhs_scale=gs_plane[:, cols], start=True, stop=True)
            key_grad = new_tile("key_grad%d_%d" % (c, first), [P, count], F32)
            nc.scalar.copy(out=key_grad[:], in_=bank[:])
            nc.vector.tensor_copy(windows[c][:].indirect(places[:, first // 16:(first + count) // 16]), key_grad[:])

        scatter_key_grad(0, 0, I // 2, "score_bank0")
        scatter_key_grad(0, I // 2, I // 2, "grad_bank1")
        scatter_key_grad(1, 0, I, "score_bank1")
        scatter_key_grad(2, 0, I, "grad_bank0")
        scatter_key_grad(3, 0, I, "score_bank0")

        fade_bank = ps.tile([P, 2, PAIR, P], F32, name="turn_bank3")
        nc.tensor.transpose(fade_bank[:, 0, 0, :], fade_rows[:], ident[:])
        fade_col = new_tile("fade_col", [P, BLOCKS], F32)
        nc.scalar.copy(out=fade_col[:], in_=fade_bank[:, 0, 0, 0:BLOCKS])

        holds = [["helped1", "qrows0_plane"], ["qrows0_codes", None]]
        faded = [[new_tile("faded%d_%d" % (pair, half), [P, 4, PAIR, P], F32, tag=holds[pair][half]) for half in range(2)]
                 for pair in range(2)]
        results = [new_tile("result%d" % c, [P, U], F32) for c in range(D // P)]

        def fade_half(pair, half, bank_names):
            for n in range(2):
                m0 = 4 * half + 2 * n
                bank = ps.tile([P, 2, PAIR, P], F32, name=bank_names[n])
                for a in range(2):
                    for b in range(PAIR):
                        nc.tensor.transpose(bank[:, a, b, :], olds[PAIR * pair + b][:, (m0 + a) * P:(m0 + a + 1) * P], ident[:])
                for a in range(2):
                    nc.scalar.activation(out=faded[pair][half][:, 2 * n + a, :, :], in_=bank[:, a, :, :], func=ACT.Copy,
                                         scale=fade_col[:, m0 + a:m0 + a + 1])

        def store(queue, c, cols):
            queue.dma_start(out=out[c * P:(c + 1) * P, cols], in_=results[c][:, cols])

        def add_on_vector(c, half, bank_name):
            bank = ps.tile([P, 4, P], F32, name=bank_name)
            for a in range(4):
                nc.tensor.transpose(bank[:, a, :], faded[c // PAIR][half][:, a, c % PAIR, :], ident[:])
            cols = slice(half * U // 2, (half + 1) * U // 2)
            nc.vector.tensor_tensor(out=results[c][:, cols], in0=bank[:].rearrange("p a n -> p (a n)"),
                                    in1=windows[c][:, cols], op=ALU.add)
            store(nc.sync, c, cols)

        def turn_window(c, bank_names):
            turned = new_tile("turned%d" % c, [P, BLOCKS, P], F32)
            for half in range(2):
                bank = ps.tile([P, 4, P], F32, name=bank_names[half])
                for a in range(4):
                    m = 4 * half + a
                    nc.tensor.transpose(bank[:, a, :], windows[c][:, m * P:(m + 1) * P], ident[:])
                nc.scalar.copy(out=turned[:, 4 * half:4 * half + 4, :], in_=bank[:])
            return turned

        def add_in_psum(c, turned, bank_names):
            for half in range(2):
                bank = ps.tile([P, 4, P], F32, name=bank_names[half])
                for a in range(4):
                    m = 4 * half + a
                    nc.tensor.matmul(bank[:, a, :], faded[c // PAIR][half][:, a, c % PAIR, :], ident[:], is_transpose=True,
                                     start=True, stop=False)
                    nc.tensor.matmul(bank[:, a, :], turned[:, m, :], ident[:], is_transpose=True, start=False, stop=True)
                cols = slice(half * U // 2, (half + 1) * U // 2)
                nc.scalar.copy(out=results[c][:, cols], in_=bank[:].rearrange("p a n -> p (a n)"))
                store(nc.scalar, c, cols)

        turn = ["turn_bank%d" % n for n in range(4)]
        fade_half(0, 0, turn[:2])
        fade_half(0, 1, turn[2:])
        fade_half(1, 0, turn[:2])
        turned0 = turn_window(0, turn[:2])
        fade_half(1, 1, turn[2:])
        add_in_psum(0, turned0, ["grad_bank0", "score_bank0"])
        add_on_vector(1, 0, "grad_bank1")
        add_on_vector(1, 1, "score_bank1")
        add_on_vector(2, 0, turn[2])
        add_on_vector(3, 0, turn[3])
        add_on_vector(2, 1, turn[0])
        add_on_vector(3, 1, turn[1])
